import numpy as np, ml_dtypes
CORES = [120,124,248,252,376,380,504,508]
N = 8
import mx_ref
NC, KT, G, WT = 128, 1, 2, 1
C = np.float32(0.041)
BF = ml_dtypes.bfloat16
def cut(t, i, w=512):
    return t[:, w * i:w * i + w]
def tile(rs):
    return np.stack(rs, axis=2).reshape(128, -1).astype(BF)
def layer(w, X):
    out = []
    for i in range(G):
        for t in range(len(X)):
            p = mx_ref.matmul(mx_ref.quantize(cut(w, len(X) * i + t)), X[t])
            z = p if t == 0 else z + p
        out.append(z)
    return out
def act(Z):
    return [np.maximum(s * z, 0) * C for z in Z for s in (1, -1)]
def setup_inputs(rng):
    def f(*shape):
        return mx_ref.flush((rng.standard_normal(shape, dtype=np.float32) * np.exp2(rng.integers(-2, 3, shape[:-1] + (1,)))).astype(BF))
    return {"x": f(N, 128, KT * 4 * NC), "w1": f(N, 128, G * KT * 512), "w2": f(N, 128, WT * 512)}
def setup_inputs_blocks(rng):
    d = setup_inputs(rng)
    for k in ("x", "w1", "w2"): d[k] = mx_ref.spread(d[k], rng, 4)
    return d
def setup_inputs_wide(rng):
    d = setup_inputs(rng)
    for k in ("x", "w1", "w2"): d[k] = mx_ref.flush((d[k].astype(np.float32) * np.exp2(rng.integers(-8, 9, (N, 1, 1))).astype(np.float32)).astype(BF))
    return d
def setup_inputs_zeros(rng):
    d = setup_inputs(rng); v = d["x"].reshape(N, 128, -1, 4).copy()
    v[np.broadcast_to((rng.random((N, 1, v.shape[2], 1)) < 0.33), v.shape)] = 0
    d["x"] = v.reshape(d["x"].shape)
    return d
def reference(x, w1, w2):
    H = [mx_ref.quantize(tile(act(layer(w1[j], [mx_ref.quantize(cut(x[j], t, 4 * NC)) for t in range(KT)])))) for j in range(N)]
    y = np.zeros((N, 128, N * WT * NC), np.float32)
    for r in range(N):
        for i in range(WT):
            qw = mx_ref.quantize(cut(w2[r], i))
            for j in range(N):
                y[r][:, NC * (WT * j + i):NC * (WT * j + i) + NC] = mx_ref.matmul(qw, H[j])
    return {"y": y}

@@ -1,0 +1,186 @@
+import numpy as np
+from concourse.bass import DstId, RemoteDMATransfer
+from concourse.mybir import dt, AluOpType, ActivationFunctionType
+
+NR = 8
+NC = 128
+C = float(np.float32(0.041))
+
+SCRATCH = {
+    "xb": ("sbuf", [128, 4 * NC], "bfloat16"),
+    "w1b": ("sbuf", [128, 8 * NC], "bfloat16"),
+    "w2b": ("sbuf", [128, 4 * NC], "bfloat16"),
+    "ht": ("sbuf", [128, 4 * NC], "bfloat16"),
+    "xc": ("sbuf", [128, NC], "float8_e4m3fn_x4"),
+    "xs": ("sbuf", [128, NC], "uint8"),
+    "w1c": ("sbuf", [128, 2 * NC], "float8_e4m3fn_x4"),
+    "w1s": ("sbuf", [128, 2 * NC], "uint8"),
+    "w2c": ("sbuf", [128, NC], "float8_e4m3fn_x4"),
+    "w2s": ("sbuf", [128, NC], "uint8"),
+    "hc": ("sbuf", [128, NR * NC], "float8_e4m3fn_x4"),
+    "hs": ("sbuf", [128, NR * NC], "uint8"),
+    "yb": ("sbuf", [128, NR * NC], "float32"),
+    "ps": ("psum", [128, 8 * 512], "float32"),
+}
+SEMAPHORES = (["ldx", "ldw1", "ldw2", "qx", "qw10", "qw11", "qh", "qw2", "z0", "z1", "r01", "r23", "sent", "st", "stl"]
+              + ["c%d" % j for j in range(NR)]
+              + ["s%d" % j for j in range(NR)]
+              + ["mm%d" % i for i in range(NR)]
+              + ["cp%d" % i for i in range(NR)])
+
+
+def rank_program(g, core, T, topo):
+    rank = T.rank_of(core)
+    if rank is None:
+        return
+    sem = T.sem
+    cores = list(T.cores)
+
+    def sib(c):
+        return [d for d in cores if d != c and topo.host(d) == topo.host(c)][0]
+
+    def same_die(c):
+        return [d for d in cores if topo.host(d) != topo.host(c) and topo.die(d) == topo.die(c)]
+
+    def in_rack(c):
+        return [d for d in same_die(c) if topo.rack(topo.host(d)) == topo.rack(topo.host(c))][0]
+
+    def cabled(c):
+        return [d for d in same_die(c) if topo.rack(topo.host(d)) != topo.rack(topo.host(c)) and topo.may_write(c, d)][0]
+
+    def diag(c):
+        return [d for d in same_die(c) if not topo.may_write(c, d)][0]
+
+    def first(c):
+        return in_rack(c) if topo.die(c) == topo.die(cores[0]) else cabled(c)
+
+    def second(c):
+        return cabled(c) if topo.die(c) == topo.die(cores[0]) else in_rack(c)
+
+    me, sb = core, sib(core)
+    fst, snd, dg = first(me), second(me), diag(me)
+    off = topo.mask(me, fst) & topo.mask(me, snd)
+    chip_all = topo.mask(me, sb)
+    on = chip_all & ~off
+
+    def cnt(m):
+        return bin(m).count("1")
+
+    def rk(c):
+        return T.rank_of(c)
+
+    def blk(j):
+        return slice(NC * j, NC * j + NC)
+
+    def codes(j):
+        return T.hc[:, NC * j:NC * j + NC].bitcast(dt.uint8)
+
+    def scales(j):
+        return T.hs[:, NC * j:NC * j + NC]
+
+    def did(d):
+        rid, pid = topo.addr(d, me)
+        return DstId(rid=rid, pnc=pid)
+
+    def bank(k):
+        return T.ps[:, 512 * k:512 * k + NC]
+
+    g.sync.dma_start(T.xb[:], T.x[:]).then_inc(sem.ldx, 16)
+    g.scalar.dma_start(T.w1b[:], T.w1[:]).then_inc(sem.ldw1, 16)
+    g.sync.wait_ge(sem.ldw1, 16)
+    g.sync.dma_start(T.w2b[:], T.w2[:]).then_inc(sem.ldw2, 16)
+
+    v = g.vector
+    v.wait_ge(sem.ldx, 16)
+    v.quantize_mx(T.xc[:], T.xs[:], T.xb[:]).then_inc(sem.qx, 1)
+    v.wait_ge(sem.ldw1, 16)
+    for i in range(2):
+        v.quantize_mx(T.w1c[:, blk(i)], T.w1s[:, blk(i)], T.w1b[:, 4 * NC * i:4 * NC * (i + 1)]).then_inc(sem["qw1%d" % i], 1)
+    t = g.tensor
+    t.wait_ge(sem.qx, 1)
+    for i in range(2):
+        t.wait_ge(sem["qw1%d" % i], 1)
+        t.matmul_mx(bank(6 + i), T.w1c[:, blk(i)], T.w1s[:, blk(i)], T.xc[:], T.xs[:], True, True).then_inc(sem["z%d" % i], 1)
+    g.scalar.wait_ge(sem.z0, 1)
+    for b, s in ((0, C), (1, -C)):
+        g.scalar.activation(T.ht[:, b:4 * NC:4], bank(6), ActivationFunctionType.Relu, scale=s).then_inc(sem.r01, 1)
+    v.wait_ge(sem.z1, 1)
+    for b, s in ((2, C), (3, -C)):
+        v.tensor_scalar(T.ht[:, b:4 * NC:4], bank(7), s, 0.0, AluOpType.mult, AluOpType.max).then_inc(sem.r23, 1)
+    v.wait_ge(sem.r01, 2)
+    v.wait_ge(sem.r23, 2)
+    v.quantize_mx(T.hc[:, blk(rank)], T.hs[:, blk(rank)], T.ht[:]).then_inc(sem.qh, 1)
+    v.wait_ge(sem.ldw2, 16)
+    v.quantize_mx(T.w2c[:], T.w2s[:], T.w2b[:]).then_inc(sem.qw2, 1)
+
+    sent = [0]
+
+    def send(*parts):
+        tr = []
+        for kind, j, dsts, m in parts:
+            ap = codes if kind == "c" else scales
+            tr.append(RemoteDMATransfer(dst_ids=[did(d) for d in dsts], dma_engine_mask=m, remote_sem=sem["%s%d" % (kind, j)],
+                                        srcs=[ap(j)], dsts=[ap(j) for _ in dsts]))
+            sent[0] += cnt(m)
+        g.remote_dma_fused(tr, local_sem=sem.sent)
+
+    ja, jb, jd = rk(fst), rk(snd), rk(dg)
+    n_off, n_on, n_all = cnt(off), cnt(on), cnt(chip_all)
+    g.wait_ge(sem.qh, 1)
+    send(("c", rank, [fst], off))
+    send(("s", rank, [fst], off))
+    send(("c", rank, [snd], off), ("c", rank, [sb], on))
+    send(("s", rank, [snd], off), ("s", rank, [sb], on))
+    g.wait_ge(sem["c%d" % ja], n_off)
+    send(("c", ja, [snd], off), ("c", ja, [sb], on))
+    g.wait_ge(sem["s%d" % ja], n_off)
+    send(("s", ja, [snd, sib(snd)], off), ("s", ja, [sb], on))
+    g.wait_ge(sem["c%d" % jb], n_off)
+    g.wait_ge(sem["s%d" % jb], n_off)
+    send(("c", jb, [sb], on))
+    send(("s", jb, [sb], on))
+    g.wait_ge(sem["c%d" % jd], n_off)
+    send(("c", jd, [sb], chip_all))
+    g.wait_ge(sem.sent, sent[0])
+
+    order = [
+        (rank, 0, 0),
+        (rk(sb), n_on, n_on),
+        (ja, n_off, n_off),
+        (jb, n_off, n_off),
+        (rk(first(sb)), n_on, n_on),
+        (jd, n_off, n_off),
+        (rk(second(sb)), n_on, n_on),
+        (rk(diag(sb)), n_all, n_off),
+    ]
+    by_scalar = (3, 6)
+    t.wait_ge(sem.qw2, 1)
+    for i, (j, nc, ns) in enumerate(order):
+        if j == rank:
+            t.wait_ge(sem.qh, 1)
+        else:
+            t.wait_ge(sem["c%d" % j], nc)
+            t.wait_ge(sem["s%d" % j], ns)
+        t.matmul_mx(bank(i), T.w2c[:], T.w2s[:], T.hc[:, blk(j)], T.hs[:, blk(j)], True, True).then_inc(sem["mm%d" % i], 1)
+        if i in by_scalar:
+            g.scalar.wait_ge(sem["mm%d" % i], 1)
+            g.scalar.activation(T.yb[:, blk(j)], bank(i), ActivationFunctionType.Copy).then_inc(sem["cp%d" % i], 1)
+        else:
+            v.wait_ge(sem["mm%d" % i], 1)
+            v.tensor_copy(T.yb[:, blk(j)], bank(i)).then_inc(sem["cp%d" % i], 1)
+
+    pos = {j: i for i, (j, nc, ns) in enumerate(order)}
+
+    def store(q, js, s):
+        for j in js:
+            q.wait_ge(sem["cp%d" % pos[j]], 1)
+        a, b = min(js), max(js) + 1
+        q.dma_start(T.y[:, NC * a:NC * b], T.yb[:, NC * a:NC * b]).then_inc(s, 16)
+
+    store(g.sync, (rank, rk(sb)), sem.st)
+    store(g.sync, (jb, rk(sib(snd))), sem.st)
+    store(g.sync, (jd,), sem.st)
+    store(g.sync, (ja, rk(sib(fst))), sem.st)
+    store(g.scalar, (rk(diag(sb)),), sem.stl)
+    g.sync.wait_ge(sem.st, 64)
+    g.scalar.wait_ge(sem.stl, 16)

@@ -5,6 +5,7 @@ from concourse.mybir import dt, AluOpType, ActivationFunctionType
 NR = 8
 NC = 128
 C = float(np.float32(0.041))
+PIECE = {"q": (0, 32), "a": (32, 80), "b": (80, 128), "c": (0, 128)}
 
 SCRATCH = {
     "xb": ("sbuf", [128, 4 * NC], "bfloat16"),
@@ -22,9 +23,8 @@ SCRATCH = {
     "yb": ("sbuf", [128, NR * NC], "float32"),
     "ps": ("psum", [128, 8 * 512], "float32"),
 }
-SEMAPHORES = (["ldx", "ldw1", "ldw2", "qx", "qw10", "qw11", "qh", "qw2", "z0", "z1", "r01", "r23", "sent", "st", "stl"]
-              + ["c%d" % j for j in range(NR)]
-              + ["s%d" % j for j in range(NR)]
+SEMAPHORES = (["ldx", "ldw10", "ldw11", "ldw2", "qx", "qw10", "qw11", "qh", "qw2", "z0", "z1", "r01", "r23", "sent", "st", "stl"]
+              + ["%s%d" % (k, j) for k in "sqabc" for j in range(NR)]
               + ["mm%d" % i for i in range(NR)]
               + ["cp%d" % i for i in range(NR)])
 
@@ -51,17 +51,9 @@ def rank_program(g, core, T, topo):
     def diag(c):
         return [d for d in same_die(c) if not topo.may_write(c, d)][0]
 
-    def first(c):
-        return in_rack(c) if topo.die(c) == topo.die(cores[0]) else cabled(c)
-
-    def second(c):
-        return cabled(c) if topo.die(c) == topo.die(cores[0]) else in_rack(c)
-
-    me, sb = core, sib(core)
-    fst, snd, dg = first(me), second(me), diag(me)
-    off = topo.mask(me, fst) & topo.mask(me, snd)
-    chip_all = topo.mask(me, sb)
-    on = chip_all & ~off
+    def deal(m):
+        bits = [1 << k for k in range(m.bit_length()) if m >> k & 1]
+        return sum(bits[0::2]), sum(bits[1::2])
 
     def cnt(m):
         return bin(m).count("1")
@@ -69,14 +61,22 @@ def rank_program(g, core, T, topo):
     def rk(c):
         return T.rank_of(c)
 
+    me, sb = core, sib(core)
+    rack, cab = in_rack(me), cabled(me)
+    off = topo.mask(me, rack) & topo.mask(me, cab)
+    chip_all = topo.mask(me, sb)
+    e_rack, e_cab = deal(off)
+    e_on0, e_on1 = deal(chip_all & ~off)
+    e_all0, e_all1 = deal(chip_all)
+
     def blk(j):
         return slice(NC * j, NC * j + NC)
 
-    def codes(j):
-        return T.hc[:, NC * j:NC * j + NC].bitcast(dt.uint8)
-
-    def scales(j):
-        return T.hs[:, NC * j:NC * j + NC]
+    def view(kind, j):
+        if kind == "s":
+            return T.hs[:, NC * j:NC * j + NC]
+        lo, hi = PIECE[kind]
+        return T.hc[:, NC * j + lo:NC * j + hi].bitcast(dt.uint8)
 
     def did(d):
         rid, pid = topo.addr(d, me)
@@ -86,15 +86,17 @@ def rank_program(g, core, T, topo):
         return T.ps[:, 512 * k:512 * k + NC]
 
     g.sync.dma_start(T.xb[:], T.x[:]).then_inc(sem.ldx, 16)
-    g.scalar.dma_start(T.w1b[:], T.w1[:]).then_inc(sem.ldw1, 16)
-    g.sync.wait_ge(sem.ldw1, 16)
+    g.scalar.dma_start(T.w1b[:, 0:4 * NC], T.w1[:, 0:4 * NC]).then_inc(sem.ldw10, 16)
+    g.sync.dma_start(T.w1b[:, 4 * NC:8 * NC], T.w1[:, 4 * NC:8 * NC]).then_inc(sem.ldw11, 16)
+    g.sync.wait_ge(sem.ldw10, 16)
+    g.sync.wait_ge(sem.ldw11, 16)
     g.sync.dma_start(T.w2b[:], T.w2[:]).then_inc(sem.ldw2, 16)
 
     v = g.vector
     v.wait_ge(sem.ldx, 16)
     v.quantize_mx(T.xc[:], T.xs[:], T.xb[:]).then_inc(sem.qx, 1)
-    v.wait_ge(sem.ldw1, 16)
     for i in range(2):
+        v.wait_ge(sem["ldw1%d" % i], 16)
         v.quantize_mx(T.w1c[:, blk(i)], T.w1s[:, blk(i)], T.w1b[:, 4 * NC * i:4 * NC * (i + 1)]).then_inc(sem["qw1%d" % i], 1)
     t = g.tensor
     t.wait_ge(sem.qx, 1)
@@ -118,49 +120,54 @@ def rank_program(g, core, T, topo):
     def send(*parts):
         tr = []
         for kind, j, dsts, m in parts:
-            ap = codes if kind == "c" else scales
+            ap = view(kind, j)
             tr.append(RemoteDMATransfer(dst_ids=[did(d) for d in dsts], dma_engine_mask=m, remote_sem=sem["%s%d" % (kind, j)],
-                                        srcs=[ap(j)], dsts=[ap(j) for _ in dsts]))
+                                        srcs=[ap], dsts=[ap for _ in dsts]))
             sent[0] += cnt(m)
         g.remote_dma_fused(tr, local_sem=sem.sent)
 
-    ja, jb, jd = rk(fst), rk(snd), rk(dg)
-    n_off, n_on, n_all = cnt(off), cnt(on), cnt(chip_all)
+    def need(q, kinds, j, n):
+        for k in kinds:
+            q.wait_ge(sem["%s%d" % (k, j)], n)
+
+    jr, jc, jd = rk(rack), rk(cab), rk(diag(me))
+    n_off, n_on, n_all = cnt(e_rack), cnt(e_on0), cnt(e_all0)
     g.wait_ge(sem.qh, 1)
-    send(("c", rank, [fst], off))
-    send(("s", rank, [fst], off))
-    send(("c", rank, [snd], off), ("c", rank, [sb], on))
-    send(("s", rank, [snd], off), ("s", rank, [sb], on))
-    g.wait_ge(sem["c%d" % ja], n_off)
-    send(("c", ja, [snd], off), ("c", ja, [sb], on))
-    g.wait_ge(sem["s%d" % ja], n_off)
-    send(("s", ja, [snd, sib(snd)], off), ("s", ja, [sb], on))
-    g.wait_ge(sem["c%d" % jb], n_off)
-    g.wait_ge(sem["s%d" % jb], n_off)
-    send(("c", jb, [sb], on))
-    send(("s", jb, [sb], on))
-    g.wait_ge(sem["c%d" % jd], n_off)
-    send(("c", jd, [sb], chip_all))
+    send(("s", rank, [rack], e_rack), ("q", rank, [cab], e_cab))
+    send(("a", rank, [rack], e_rack), ("b", rank, [cab], e_cab))
+    send(("b", rank, [rack], e_rack), ("a", rank, [cab], e_cab), ("a", rank, [sb], e_on0), ("b", rank, [sb], e_on1))
+    send(("q", rank, [rack], e_rack), ("s", rank, [cab], e_cab), ("q", rank, [sb], e_on0), ("s", rank, [sb], e_on1))
+    need(g, "s", jr, n_off)
+    need(g, "q", jc, n_off)
+    send(("q", jc, [rack], e_rack), ("s", jr, [cab], e_cab))
+    need(g, "a", jr, n_off)
+    need(g, "b", jc, n_off)
+    send(("b", jc, [rack, sib(rack)], e_rack), ("a", jr, [cab, sib(cab)], e_cab))
+    need(g, "qb", jr, n_off)
+    need(g, "qa", jc, n_off)
+    send(("c", jr, [sb], e_on0), ("c", jc, [sb], e_on1))
+    need(g, "s", jc, n_off)
+    send(("s", jr, [sb], e_on0), ("s", jc, [sb], e_on1))
+    need(g, "sq", jd, n_off)
+    send(("s", jd, [sb], e_all0), ("q", jd, [sb], e_all1))
     g.wait_ge(sem.sent, sent[0])
 
     order = [
-        (rank, 0, 0),
-        (rk(sb), n_on, n_on),
-        (ja, n_off, n_off),
-        (jb, n_off, n_off),
-        (rk(first(sb)), n_on, n_on),
-        (jd, n_off, n_off),
-        (rk(second(sb)), n_on, n_on),
-        (rk(diag(sb)), n_all, n_off),
+        (rank, ()),
+        (rk(sb), (("sqab", n_on),)),
+        (jr, (("sqab", n_off),)),
+        (jc, (("sqab", n_off),)),
+        (rk(in_rack(sb)), (("sc", n_on),)),
+        (rk(cabled(sb)), (("sc", n_on),)),
+        (jd, (("sqab", n_off),)),
+        (rk(diag(sb)), (("ab", n_off), ("sq", n_all))),
     ]
     by_scalar = (3, 6)
+    t.wait_ge(sem.qh, 1)
     t.wait_ge(sem.qw2, 1)
-    for i, (j, nc, ns) in enumerate(order):
-        if j == rank:
-            t.wait_ge(sem.qh, 1)
-        else:
-            t.wait_ge(sem["c%d" % j], nc)
-            t.wait_ge(sem["s%d" % j], ns)
+    for i, (j, waits) in enumerate(order):
+        for kinds, n in waits:
+            need(t, kinds, j, n)
         t.matmul_mx(bank(i), T.w2c[:], T.w2s[:], T.hc[:, blk(j)], T.hs[:, blk(j)], True, True).then_inc(sem["mm%d" % i], 1)
         if i in by_scalar:
             g.scalar.wait_ge(sem["mm%d" % i], 1)
@@ -169,7 +176,7 @@ def rank_program(g, core, T, topo):
             v.wait_ge(sem["mm%d" % i], 1)
             v.tensor_copy(T.yb[:, blk(j)], bank(i)).then_inc(sem["cp%d" % i], 1)
 
-    pos = {j: i for i, (j, nc, ns) in enumerate(order)}
+    pos = {j: i for i, (j, waits) in enumerate(order)}
 
     def store(q, js, s):
         for j in js:
@@ -178,9 +185,9 @@ def rank_program(g, core, T, topo):
         q.dma_start(T.y[:, NC * a:NC * b], T.yb[:, NC * a:NC * b]).then_inc(s, 16)
 
     store(g.sync, (rank, rk(sb)), sem.st)
-    store(g.sync, (jb, rk(sib(snd))), sem.st)
-    store(g.sync, (jd,), sem.st)
-    store(g.sync, (ja, rk(sib(fst))), sem.st)
-    store(g.scalar, (rk(diag(sb)),), sem.stl)
+    store(g.sync, (jr, rk(in_rack(sb))), sem.st)
+    store(g.sync, (jc, rk(cabled(sb))), sem.st)
+    store(g.scalar, (jd,), sem.stl)
+    store(g.sync, (rk(diag(sb)),), sem.st)
     g.sync.wait_ge(sem.st, 64)
     g.scalar.wait_ge(sem.stl, 16)

import numpy as np
from concourse.bass import DstId, RemoteDMATransfer
from concourse.mybir import dt, AluOpType, ActivationFunctionType

NR = 8
NC = 128
C = float(np.float32(0.041))
PIECE = {"q": (0, 32), "a": (32, 80), "b": (80, 128), "c": (0, 128)}

SCRATCH = {
    "xb": ("sbuf", [128, 4 * NC], "bfloat16"),
    "w1b": ("sbuf", [128, 8 * NC], "bfloat16"),
    "w2b": ("sbuf", [128, 4 * NC], "bfloat16"),
    "ht": ("sbuf", [128, 4 * NC], "bfloat16"),
    "xc": ("sbuf", [128, NC], "float8_e4m3fn_x4"),
    "xs": ("sbuf", [128, NC], "uint8"),
    "w1c": ("sbuf", [128, 2 * NC], "float8_e4m3fn_x4"),
    "w1s": ("sbuf", [128, 2 * NC], "uint8"),
    "w2c": ("sbuf", [128, NC], "float8_e4m3fn_x4"),
    "w2s": ("sbuf", [128, NC], "uint8"),
    "hc": ("sbuf", [128, NR * NC], "float8_e4m3fn_x4"),
    "hs": ("sbuf", [128, NR * NC], "uint8"),
    "yb": ("sbuf", [128, NR * NC], "float32"),
    "ps": ("psum", [128, 8 * 512], "float32"),
}
SEMAPHORES = (["ldx", "ldw10", "ldw11", "ldw2", "qx", "qw10", "qw11", "qh", "qw2", "z0", "z1", "r01", "r23", "sent", "st", "stl"]
              + ["%s%d" % (k, j) for k in "sqabc" for j in range(NR)]
              + ["mm%d" % i for i in range(NR)]
              + ["cp%d" % i for i in range(NR)])


def rank_program(g, core, T, topo):
    rank = T.rank_of(core)
    if rank is None:
        return
    sem = T.sem
    cores = list(T.cores)

    def sib(c):
        return [d for d in cores if d != c and topo.host(d) == topo.host(c)][0]

    def same_die(c):
        return [d for d in cores if topo.host(d) != topo.host(c) and topo.die(d) == topo.die(c)]

    def in_rack(c):
        return [d for d in same_die(c) if topo.rack(topo.host(d)) == topo.rack(topo.host(c))][0]

    def cabled(c):
        return [d for d in same_die(c) if topo.rack(topo.host(d)) != topo.rack(topo.host(c)) and topo.may_write(c, d)][0]

    def diag(c):
        return [d for d in same_die(c) if not topo.may_write(c, d)][0]

    def deal(m):
        bits = [1 << k for k in range(m.bit_length()) if m >> k & 1]
        return sum(bits[0::2]), sum(bits[1::2])

    def cnt(m):
        return bin(m).count("1")

    def rk(c):
        return T.rank_of(c)

    me, sb = core, sib(core)
    rack, cab = in_rack(me), cabled(me)
    off = topo.mask(me, rack) & topo.mask(me, cab)
    chip_all = topo.mask(me, sb)
    e_rack, e_cab = deal(off)
    e_on0, e_on1 = deal(chip_all & ~off)
    e_all0, e_all1 = deal(chip_all)

    def blk(j):
        return slice(NC * j, NC * j + NC)

    def view(kind, j):
        if kind == "s":
            return T.hs[:, NC * j:NC * j + NC]
        lo, hi = PIECE[kind]
        return T.hc[:, NC * j + lo:NC * j + hi].bitcast(dt.uint8)

    def did(d):
        rid, pid = topo.addr(d, me)
        return DstId(rid=rid, pnc=pid)

    def bank(k):
        return T.ps[:, 512 * k:512 * k + NC]

    g.sync.dma_start(T.xb[:], T.x[:]).then_inc(sem.ldx, 16)
    g.scalar.dma_start(T.w1b[:, 0:4 * NC], T.w1[:, 0:4 * NC]).then_inc(sem.ldw10, 16)
    g.sync.dma_start(T.w1b[:, 4 * NC:8 * NC], T.w1[:, 4 * NC:8 * NC]).then_inc(sem.ldw11, 16)
    g.sync.wait_ge(sem.ldw10, 16)
    g.sync.wait_ge(sem.ldw11, 16)
    g.sync.dma_start(T.w2b[:], T.w2[:]).then_inc(sem.ldw2, 16)

    v = g.vector
    v.wait_ge(sem.ldx, 16)
    v.quantize_mx(T.xc[:], T.xs[:], T.xb[:]).then_inc(sem.qx, 1)
    for i in range(2):
        v.wait_ge(sem["ldw1%d" % i], 16)
        v.quantize_mx(T.w1c[:, blk(i)], T.w1s[:, blk(i)], T.w1b[:, 4 * NC * i:4 * NC * (i + 1)]).then_inc(sem["qw1%d" % i], 1)
    t = g.tensor
    t.wait_ge(sem.qx, 1)
    for i in range(2):
        t.wait_ge(sem["qw1%d" % i], 1)
        t.matmul_mx(bank(6 + i), T.w1c[:, blk(i)], T.w1s[:, blk(i)], T.xc[:], T.xs[:], True, True).then_inc(sem["z%d" % i], 1)
    g.scalar.wait_ge(sem.z0, 1)
    for b, s in ((0, C), (1, -C)):
        g.scalar.activation(T.ht[:, b:4 * NC:4], bank(6), ActivationFunctionType.Relu, scale=s).then_inc(sem.r01, 1)
    v.wait_ge(sem.z1, 1)
    for b, s in ((2, C), (3, -C)):
        v.tensor_scalar(T.ht[:, b:4 * NC:4], bank(7), s, 0.0, AluOpType.mult, AluOpType.max).then_inc(sem.r23, 1)
    v.wait_ge(sem.r01, 2)
    v.wait_ge(sem.r23, 2)
    v.quantize_mx(T.hc[:, blk(rank)], T.hs[:, blk(rank)], T.ht[:]).then_inc(sem.qh, 1)
    v.wait_ge(sem.ldw2, 16)
    v.quantize_mx(T.w2c[:], T.w2s[:], T.w2b[:]).then_inc(sem.qw2, 1)

    sent = [0]

    def send(*parts):
        tr = []
        for kind, j, dsts, m in parts:
            ap = view(kind, j)
            tr.append(RemoteDMATransfer(dst_ids=[did(d) for d in dsts], dma_engine_mask=m, remote_sem=sem["%s%d" % (kind, j)],
                                        srcs=[ap], dsts=[ap for _ in dsts]))
            sent[0] += cnt(m)
        g.remote_dma_fused(tr, local_sem=sem.sent)

    def need(q, kinds, j, n):
        for k in kinds:
            q.wait_ge(sem["%s%d" % (k, j)], n)

    jr, jc, jd = rk(rack), rk(cab), rk(diag(me))
    n_off, n_on, n_all = cnt(e_rack), cnt(e_on0), cnt(e_all0)
    g.wait_ge(sem.qh, 1)
    send(("s", rank, [rack], e_rack), ("q", rank, [cab], e_cab))
    send(("a", rank, [rack], e_rack), ("b", rank, [cab], e_cab))
    send(("b", rank, [rack], e_rack), ("a", rank, [cab], e_cab), ("a", rank, [sb], e_on0), ("b", rank, [sb], e_on1))
    send(("q", rank, [rack], e_rack), ("s", rank, [cab], e_cab), ("q", rank, [sb], e_on0), ("s", rank, [sb], e_on1))
    need(g, "s", jr, n_off)
    need(g, "q", jc, n_off)
    send(("q", jc, [rack], e_rack), ("s", jr, [cab], e_cab))
    need(g, "a", jr, n_off)
    need(g, "b", jc, n_off)
    send(("b", jc, [rack, sib(rack)], e_rack), ("a", jr, [cab, sib(cab)], e_cab))
    need(g, "qb", jr, n_off)
    need(g, "qa", jc, n_off)
    send(("c", jr, [sb], e_on0), ("c", jc, [sb], e_on1))
    need(g, "s", jc, n_off)
    send(("s", jr, [sb], e_on0), ("s", jc, [sb], e_on1))
    need(g, "sq", jd, n_off)
    send(("s", jd, [sb], e_all0), ("q", jd, [sb], e_all1))
    g.wait_ge(sem.sent, sent[0])

    order = [
        (rank, ()),
        (rk(sb), (("sqab", n_on),)),
        (jr, (("sqab", n_off),)),
        (jc, (("sqab", n_off),)),
        (rk(in_rack(sb)), (("sc", n_on),)),
        (rk(cabled(sb)), (("sc", n_on),)),
        (jd, (("sqab", n_off),)),
        (rk(diag(sb)), (("ab", n_off), ("sq", n_all))),
    ]
    by_scalar = (3, 6)
    t.wait_ge(sem.qh, 1)
    t.wait_ge(sem.qw2, 1)
    for i, (j, waits) in enumerate(order):
        for kinds, n in waits:
            need(t, kinds, j, n)
        t.matmul_mx(bank(i), T.w2c[:], T.w2s[:], T.hc[:, blk(j)], T.hs[:, blk(j)], True, True).then_inc(sem["mm%d" % i], 1)
        if i in by_scalar:
            g.scalar.wait_ge(sem["mm%d" % i], 1)
            g.scalar.activation(T.yb[:, blk(j)], bank(i), ActivationFunctionType.Copy).then_inc(sem["cp%d" % i], 1)
        else:
            v.wait_ge(sem["mm%d" % i], 1)
            v.tensor_copy(T.yb[:, blk(j)], bank(i)).then_inc(sem["cp%d" % i], 1)

    pos = {j: i for i, (j, waits) in enumerate(order)}

    def store(q, js, s):
        for j in js:
            q.wait_ge(sem["cp%d" % pos[j]], 1)
        a, b = min(js), max(js) + 1
        q.dma_start(T.y[:, NC * a:NC * b], T.yb[:, NC * a:NC * b]).then_inc(s, 16)

    store(g.sync, (rank, rk(sb)), sem.st)
    store(g.sync, (jr, rk(in_rack(sb))), sem.st)
    store(g.sync, (jc, rk(cabled(sb))), sem.st)
    store(g.scalar, (jd,), sem.stl)
    store(g.sync, (rk(diag(sb)),), sem.st)
    g.sync.wait_ge(sem.st, 64)
    g.scalar.wait_ge(sem.stl, 16)
